import numpy as np
import ml_dtypes

BF16 = ml_dtypes.bfloat16


def bf(x):
    return np.asarray(x, np.float32).astype(BF16)


def f32(x):
    return np.asarray(x, np.float32)


def f64(x):
    return np.asarray(x).astype(np.float64)


def striped(idx):
    return np.tile(idx.reshape(-1, 16).T, (8, 1))


def rows(idx, k):
    return np.tile(idx, (k, 1))


def look(tab, idx):
    return np.take_along_axis(f64(tab), rows(idx, len(tab)), axis=1)


K, S, D, V, N, M = 512, 256, 2, 128, 256, 256


def setup_inputs():
    return {"tab": f32(np.random.standard_normal((K, S))), "ctr": f32(np.random.standard_normal((K, V))), "w": bf(np.random.standard_normal((K, M)) / np.sqrt(K)), "offs": striped(np.random.permutation(S)[:N])}


def reference(tab, ctr, w, offs):
    idx = offs[:16].T.reshape(-1)
    x = sum(np.maximum(look(tab, idx[d * V:(d + 1) * V]) - f64(ctr), 0.0) for d in range(D))
    y = f64(w).T @ x
    return y

@@ -1,0 +1,63 @@
+import concourse.mybir as mybir
+
+F32, BF16, U16 = mybir.dt.float32, mybir.dt.bfloat16, mybir.dt.uint16
+ALU = mybir.AluOpType
+RELU = mybir.ActivationFunctionType.Relu
+
+P = 128
+ROWS = 512
+S = 256
+V = 128
+M = 256
+BLOCKS = ROWS // P
+HALVES = M // P
+LIST = 2 * V // 16
+PART = V // 16
+
+FLOPS = 2 * ROWS * M * V
+
+
+def tile_lookup_edge_sub_none_kernel(tc, tab, ctr, w, offs, out):
+    nc = tc.nc
+    tab_rows = tab.rearrange("(p b) s -> p b s", b=BLOCKS)
+    ctr_rows = ctr.rearrange("(p b) j -> p b j", b=BLOCKS)
+    w_rows = w.rearrange("(p b) m -> p b m", b=BLOCKS)
+
+    with (
+        tc.tile_pool(name="held", bufs=1) as held,
+        tc.tile_pool(name="work", bufs=BLOCKS) as work,
+        tc.psum_pool(name="sums", bufs=1) as sums,
+    ):
+        offsets = held.tile([P, LIST], U16, name="offsets")
+        windows = [held.tile([P, S], F32, name=f"window{b}") for b in range(BLOCKS)]
+        centres = [held.tile([P, 2, V], F32, name=f"centres{h}") for h in range(2)]
+        weights = held.tile([P, BLOCKS, M], BF16, name="weights")
+
+        nc.sync.dma_start(offsets[:], offs)
+        for b in range(BLOCKS):
+            nc.sync.dma_start(windows[b][:], tab_rows[:, b, :])
+        for h in range(2):
+            nc.scalar.dma_start(centres[h][:], ctr_rows[:, 2 * h : 2 * h + 2, :])
+        nc.scalar.dma_start(weights[:], w_rows)
+
+        products = [sums.tile([P, V], F32, name=f"product{h}") for h in range(HALVES)]
+        for b in range(BLOCKS):
+            centre = centres[b // 2][:, b % 2, :]
+            first = work.tile([P, V], F32, name="first")
+            second = work.tile([P, V], F32, name="second")
+            positive = work.tile([P, V], F32, name="positive")
+            x = work.tile([P, V], BF16, name="x")
+            nc.vector.tensor_tensor(first[:], windows[b][:].indirect(offsets[:, 0:PART]), centre, ALU.subtract)
+            nc.scalar.activation(positive[:], first[:], RELU)
+            nc.vector.tensor_tensor(second[:], windows[b][:].indirect(offsets[:, PART:LIST]), centre, ALU.subtract)
+            nc.vector.scalar_tensor_tensor(x[:], second[:], 0.0, positive[:], ALU.max, ALU.add)
+            for h in range(HALVES):
+                nc.tensor.matmul(
+                    products[h][:], weights[:, b, h * P : (h + 1) * P], x[:], start=b == 0, stop=b == BLOCKS - 1
+                )
+
+        results = [held.tile([P, V], F32, name=f"result{h}") for h in range(HALVES)]
+        nc.vector.tensor_copy(results[0][:], products[0][:])
+        nc.sync.dma_start(out[0:P, :], results[0][:])
+        nc.scalar.copy(results[1][:], products[1][:])
+        nc.scalar.dma_start(out[P:M, :], results[1][:])

@@ -36,9 +36,9 @@ def tile_lookup_edge_sub_none_kernel(tc, tab, ctr, w, offs, out):
         nc.sync.dma_start(offsets[:], offs)
         for b in range(BLOCKS):
             nc.sync.dma_start(windows[b][:], tab_rows[:, b, :])
-        for h in range(2):
-            nc.scalar.dma_start(centres[h][:], ctr_rows[:, 2 * h : 2 * h + 2, :])
+        nc.scalar.dma_start(centres[0][:], ctr_rows[:, 0:2, :])
         nc.scalar.dma_start(weights[:], w_rows)
+        nc.scalar.dma_start(centres[1][:], ctr_rows[:, 2:4, :])
 
         products = [sums.tile([P, V], F32, name=f"product{h}") for h in range(HALVES)]
         for b in range(BLOCKS):

@@ -33,12 +33,18 @@ def tile_lookup_edge_sub_none_kernel(tc, tab, ctr, w, offs, out):
         centres = [held.tile([P, 2, V], F32, name=f"centres{h}") for h in range(2)]
         weights = held.tile([P, BLOCKS, M], BF16, name="weights")
 
+        column = held.tile([P, 1], F32, name="column")
+        warmed = held.tile([P, 1], F32, name="warmed")
+        nc.gpsimd.memset(column[:], 0.0)
+
         nc.sync.dma_start(offsets[:], offs)
         for b in range(BLOCKS):
             nc.sync.dma_start(windows[b][:], tab_rows[:, b, :])
         nc.scalar.dma_start(centres[0][:], ctr_rows[:, 0:2, :])
         nc.scalar.dma_start(weights[:], w_rows)
         nc.scalar.dma_start(centres[1][:], ctr_rows[:, 2:4, :])
+
+        nc.scalar.activation(warmed[:], column[:], RELU)
 
         products = [sums.tile([P, V], F32, name=f"product{h}") for h in range(HALVES)]
         for b in range(BLOCKS):

@@ -30,7 +30,8 @@ def tile_lookup_edge_sub_none_kernel(tc, tab, ctr, w, offs, out):
     ):
         offsets = held.tile([P, LIST], U16, name="offsets")
         windows = [held.tile([P, S], F32, name=f"window{b}") for b in range(BLOCKS)]
-        centres = [held.tile([P, 2, V], F32, name=f"centres{h}") for h in range(2)]
+        centre0 = held.tile([P, V], F32, name="centre0")
+        centres = held.tile([P, BLOCKS - 1, V], F32, name="centres")
         weights = held.tile([P, BLOCKS, M], BF16, name="weights")
 
         column = held.tile([P, 1], F32, name="column")
@@ -40,15 +41,15 @@ def tile_lookup_edge_sub_none_kernel(tc, tab, ctr, w, offs, out):
         nc.sync.dma_start(offsets[:], offs)
         for b in range(BLOCKS):
             nc.sync.dma_start(windows[b][:], tab_rows[:, b, :])
-        nc.scalar.dma_start(centres[0][:], ctr_rows[:, 0:2, :])
+        nc.scalar.dma_start(centre0[:], ctr_rows[:, 0, :])
+        nc.scalar.dma_start(centres[:], ctr_rows[:, 1:BLOCKS, :])
         nc.scalar.dma_start(weights[:], w_rows)
-        nc.scalar.dma_start(centres[1][:], ctr_rows[:, 2:4, :])
 
         nc.scalar.activation(warmed[:], column[:], RELU)
 
         products = [sums.tile([P, V], F32, name=f"product{h}") for h in range(HALVES)]
         for b in range(BLOCKS):
-            centre = centres[b // 2][:, b % 2, :]
+            centre = centre0[:] if b == 0 else centres[:, b - 1, :]
             first = work.tile([P, V], F32, name="first")
             second = work.tile([P, V], F32, name="second")
             positive = work.tile([P, V], F32, name="positive")

import concourse.mybir as mybir

F32, BF16, U16 = mybir.dt.float32, mybir.dt.bfloat16, mybir.dt.uint16
ALU = mybir.AluOpType
RELU = mybir.ActivationFunctionType.Relu

P = 128
ROWS = 512
S = 256
V = 128
M = 256
BLOCKS = ROWS // P
HALVES = M // P
LIST = 2 * V // 16
PART = V // 16

FLOPS = 2 * ROWS * M * V


def tile_lookup_edge_sub_none_kernel(tc, tab, ctr, w, offs, out):
    nc = tc.nc
    tab_rows = tab.rearrange("(p b) s -> p b s", b=BLOCKS)
    ctr_rows = ctr.rearrange("(p b) j -> p b j", b=BLOCKS)
    w_rows = w.rearrange("(p b) m -> p b m", b=BLOCKS)

    with (
        tc.tile_pool(name="held", bufs=1) as held,
        tc.tile_pool(name="work", bufs=BLOCKS) as work,
        tc.psum_pool(name="sums", bufs=1) as sums,
    ):
        offsets = held.tile([P, LIST], U16, name="offsets")
        windows = [held.tile([P, S], F32, name=f"window{b}") for b in range(BLOCKS)]
        centre0 = held.tile([P, V], F32, name="centre0")
        centres = held.tile([P, BLOCKS - 1, V], F32, name="centres")
        weights = held.tile([P, BLOCKS, M], BF16, name="weights")

        column = held.tile([P, 1], F32, name="column")
        warmed = held.tile([P, 1], F32, name="warmed")
        nc.gpsimd.memset(column[:], 0.0)

        nc.sync.dma_start(offsets[:], offs)
        for b in range(BLOCKS):
            nc.sync.dma_start(windows[b][:], tab_rows[:, b, :])
        nc.scalar.dma_start(centre0[:], ctr_rows[:, 0, :])
        nc.scalar.dma_start(centres[:], ctr_rows[:, 1:BLOCKS, :])
        nc.scalar.dma_start(weights[:], w_rows)

        nc.scalar.activation(warmed[:], column[:], RELU)

        products = [sums.tile([P, V], F32, name=f"product{h}") for h in range(HALVES)]
        for b in range(BLOCKS):
            centre = centre0[:] if b == 0 else centres[:, b - 1, :]
            first = work.tile([P, V], F32, name="first")
            second = work.tile([P, V], F32, name="second")
            positive = work.tile([P, V], F32, name="positive")
            x = work.tile([P, V], BF16, name="x")
            nc.vector.tensor_tensor(first[:], windows[b][:].indirect(offsets[:, 0:PART]), centre, ALU.subtract)
            nc.scalar.activation(positive[:], first[:], RELU)
            nc.vector.tensor_tensor(second[:], windows[b][:].indirect(offsets[:, PART:LIST]), centre, ALU.subtract)
            nc.vector.scalar_tensor_tensor(x[:], second[:], 0.0, positive[:], ALU.max, ALU.add)
            for h in range(HALVES):
                nc.tensor.matmul(
                    products[h][:], weights[:, b, h * P : (h + 1) * P], x[:], start=b == 0, stop=b == BLOCKS - 1
                )

        results = [held.tile([P, V], F32, name=f"result{h}") for h in range(HALVES)]
        nc.vector.tensor_copy(results[0][:], products[0][:])
        nc.sync.dma_start(out[0:P, :], results[0][:])
        nc.scalar.copy(results[1][:], products[1][:])
        nc.scalar.dma_start(out[P:M, :], results[1][:])
